import numpy as np
import ml_dtypes


def mxq(x, axis, fmt="e4m3"):
    dtype, down = {"e4m3": (ml_dtypes.float8_e4m3fn, 7), "e5m2": (ml_dtypes.float8_e5m2, 14)}[fmt]
    v = np.moveaxis(np.asarray(x, np.float32).astype(ml_dtypes.bfloat16).astype(np.float64), axis, -1)
    blocks = v.reshape(v.shape[:-1] + (-1, 32))
    amax = np.abs(blocks).max(-1, keepdims=True)
    byte = np.maximum(np.where(amax > 0, np.frexp(amax)[1] - 1 + 127, 0) - down, 1)
    scale = np.exp2(byte - 127.0)
    codes = (blocks / scale).astype(np.float32).astype(dtype).astype(np.float64)
    return np.moveaxis((codes * scale).reshape(v.shape), -1, axis)


WIDE = False


def mx_kscale(k):
    if not WIDE:
        return np.ones(k)
    levels = np.array([10, -10, 5, -5, 0])
    if k % 512:
        return np.exp2(np.random.permutation(np.resize(levels, k // 32))).repeat(32)
    a = np.empty((k // 512, 16))
    for p in range(k // 512):
        a[p, :8] = np.random.permutation(np.resize(levels, 8))
        for g in range(8):
            far = levels[np.abs(levels - a[p, g]) >= 10]
            a[p, g + 8] = far[np.random.randint(len(far))]
    return np.exp2(a.ravel()).repeat(32)


def f64(x):
    return np.asarray(x).astype(np.float64)


def striped(idx):
    return np.tile(idx.reshape(-1, 16).T, (8, 1)).astype(np.uint16)


def unstriped(offs):
    return offs[:16].T.reshape(-1).astype(np.int64)


E2M1 = np.array([0.0, 0.5, 1.0, 1.5, 2.0, 3.0, 4.0, 6.0, -0.0, -0.5, -1.0, -1.5, -2.0, -3.0, -4.0, -6.0])


def pack_weight(w, fmt):
    k, n = w.shape
    w = f64(np.asarray(w, np.float32).astype(ml_dtypes.bfloat16)).reshape(k // 32, 32, n)
    amax = np.abs(w).max(1)
    if fmt == "e4m3":
        byte = np.frexp(amax)[1] - 1 + 127 - 7
    else:
        mant, ex = np.frexp(amax / 6.0)
        byte = np.where(mant > 0.5, ex, ex - 1) + 127
    byte = np.clip(np.where(amax > 0, byte, 1), 1, 254)
    scaled = (w * np.exp2(127.0 - byte)[:, None, :]).reshape(k, n).astype(np.float32)
    by_word = np.ascontiguousarray(scaled.reshape(k // 512, 128, 4, n).transpose(0, 1, 3, 2))
    if fmt == "e4m3":
        words = by_word.astype(ml_dtypes.float8_e4m3fn).view(np.uint8)
    else:
        c = by_word.astype(ml_dtypes.float4_e2m1fn).view(np.uint8) & 0xF
        words = (c[..., 0::2] | (c[..., 1::2] << 4)).reshape(k // 512, 128, 2 * n)
    return np.ascontiguousarray(words), np.ascontiguousarray(byte.astype(np.uint8).reshape(k // 512, 16, n))


def unpack_weight(words, scales, fmt):
    g, _, n = scales.shape
    words = np.ascontiguousarray(words).reshape(g, 128, n, -1)
    if fmt == "e4m3":
        vals = words.view(ml_dtypes.float8_e4m3fn).astype(np.float64)
    else:
        nib = np.empty((g, 128, n, 4), np.uint8)
        nib[..., 0::2] = words & 0xF
        nib[..., 1::2] = words >> 4
        vals = E2M1[nib]
    vals = vals * np.repeat(np.exp2(scales.astype(np.float64) - 127.0), 8, axis=1)[..., None]
    return vals.transpose(0, 1, 3, 2).reshape(g * 512, n)


def gelu(v):
    return 0.5 * v * (1.0 + np.tanh(np.sqrt(2.0 / np.pi) * (v + 0.044715 * v**3)))


def often(T, S):
    return np.random.permutation(T)[(T * np.random.uniform(0, 1, S) ** 4).astype(np.int64)]


K, K2, H, N, T, S, P = 1024, 512, 1024, 512, 2048, 1024, 512

def setup_inputs():
    n = np.random.standard_normal
    s = mx_kscale(K)[:, None]
    s2 = mx_kscale(K2)[:, None]
    u = mx_kscale(H)[:, None]
    d = {}
    d["tab_words"], d["tab_scales"] = pack_weight(n((K, T)) * s, "e4m3")
    d["tab2_words"], d["tab2_scales"] = pack_weight(n((K2, T)) * s2, "e4m3")
    d["tab3_words"], d["tab3_scales"] = pack_weight(n((K2, T)) * s2, "e4m3")
    d["offs"] = striped(np.random.permutation(T)[:S])
    d["offs2"] = striped(np.random.permutation(T)[:S])
    d["offs3"] = striped(np.random.permutation(T)[:S])
    d["pos1"] = striped(np.random.permutation(S)[:P])
    d["pos2"] = striped(often(S, P))
    d["pos3"] = striped(often(S, P))
    d["w1"] = (n((K, H)) / s * u.T / K**0.5).astype(np.float32)
    d["w2_words"], d["w2_scales"] = pack_weight(1.3 * n((K2, H)) / s2 * u.T / K2**0.5, "e4m3")
    d["w3"] = (n((K2, H)) / s2 / K2**0.5).astype(np.float32)
    d["ask"] = (0.8 * n((H, P)) * u).astype(np.float32)
    d["keel"] = (0.8 * np.exp(0.3 * n(H)) * u[:, 0]).astype(np.float32)
    d["w4_words"], d["w4_scales"] = pack_weight(1.2 * n((H, N)) / u / H**0.5, "e2m1")
    return d

def reference(tab_words, tab_scales, tab2_words, tab2_scales, tab3_words, tab3_scales, offs, offs2, offs3, pos1, pos2, pos3, w1, w2_words, w2_scales, w3, ask, keel, w4_words, w4_scales):
    v = unpack_weight(tab_words, tab_scales, "e4m3")[:, unstriped(offs)]
    v2 = unpack_weight(tab2_words, tab2_scales, "e4m3")[:, unstriped(offs2)]
    v3 = unpack_weight(tab3_words, tab3_scales, "e4m3")[:, unstriped(offs3)]
    a = mxq(f64(w1), 0, "e4m3").T @ v
    b = unpack_weight(w2_words, w2_scales, "e4m3").T @ v2
    d = mxq(f64(w3), 0, "e4m3").T @ v3
    fit = np.minimum(a[:, unstriped(pos1)] + f64(ask), b[:, unstriped(pos2)])
    z = fit - d[:, unstriped(pos3)] * f64(keel)[:, None]
    y = unpack_weight(w4_words, w4_scales, "e2m1").T @ mxq(z, 0, "e4m3")
    return y + np.tanh(y)

@@ -1,0 +1,279 @@
+from contextlib import ExitStack
+
+import concourse.mybir as mybir
+
+K, K2, H, N, T, S, J = 1024, 512, 1024, 512, 2048, 1024, 512
+FLOPS = 2 * (K * H * S + 2 * K2 * H * S + H * N * J)
+
+F32 = mybir.dt.float32
+BF16 = mybir.dt.bfloat16
+I32 = mybir.dt.int32
+U32 = mybir.dt.uint32
+U16 = mybir.dt.uint16
+U8 = mybir.dt.uint8
+FP8X4 = mybir.dt.float8_e4m3fn_x4
+FP4X4 = mybir.dt.float4_e2m1fn_x4
+ALU = mybir.AluOpType
+ACT = mybir.ActivationFunctionType
+
+P = 128
+PACK = 4
+PASS = P * PACK
+BANK = 512
+HALF = J // 2
+
+
+def tile_list_berth_tide_features_kernel(
+    tc, tab_words, tab_scales, tab2_words, tab2_scales, tab3_words, tab3_scales,
+    offs, offs2, offs3, pos1, pos2, pos3, w1, w2_words, w2_scales, w3, ask, keel,
+    w4_words, w4_scales, out,
+):
+    nc = tc.nc
+    with ExitStack() as ctx:
+        held = ctx.enter_context(tc.tile_pool(name="held", bufs=1))
+        ring = ctx.enter_context(tc.tile_pool(name="ring", bufs=1))
+        psum = ctx.enter_context(tc.psum_pool(name="psum", bufs=4))
+
+        def keep(shape, dtype, name):
+            return held.tile(shape, dtype, name=name, align_bytes=64)
+
+        def load_list(src, name):
+            tile = held.tile(list(src.shape), U16, name=name)
+            nc.sync.dma_start(tile[:], src)
+            return tile
+
+        def zeroed_plane(engine, width, name):
+            tile = keep([P, width], U8, name)
+            engine.memset(tile[:].bitcast(I32), 0)
+            return tile
+
+        def load_scale_rows(queues, plane, scales):
+            rows = PACK * scales.shape[0]
+            for q, queue in enumerate(queues):
+                queue.dma_start(
+                    out=plane[32 * q : 32 * q + rows, :].bitcast(I32),
+                    in_=scales[:, 4 * q : 4 * q + 4, :].bitcast(I32),
+                )
+
+        def load_words(words, name):
+            tile = keep([P, words.shape[1]], I32, name)
+            nc.sync.dma_start(out=tile[:], in_=words.rearrange("p c i -> p (c i)").bitcast(I32))
+            return tile
+
+        def load_rows(rows, name):
+            tile = ring.tile([P, PACK, BANK], F32, name=name, tag="wide", bufs=5, align_bytes=64)
+            nc.sync.dma_start(out=tile[:], in_=rows.rearrange("(p j) c -> p j c", j=PACK))
+            return tile
+
+        plane2 = zeroed_plane(nc.gpsimd, T, "plane2")
+        w2_plane_raw = zeroed_plane(nc.gpsimd, H, "w2_plane_raw")
+        plane1 = zeroed_plane(nc.vector, T, "plane1")
+        plane3 = zeroed_plane(nc.vector, T, "plane3")
+        w4_plane = zeroed_plane(nc.vector, 2 * N, "w4_plane")
+
+        list2 = load_list(offs2, "list2")
+        list1 = load_list(offs, "list1")
+        load_scale_rows([nc.sync] * 4, plane2, tab2_scales)
+        words2 = load_words(tab2_words[0], "words2")
+        w2_raw = load_words(w2_words[0], "w2_raw")
+        load_scale_rows([nc.gpsimd] * 3 + [nc.sync], w2_plane_raw, w2_scales)
+        load_scale_rows([nc.sync] * 4, plane1, tab_scales)
+        words1 = [load_words(tab_words[a], "words1_%d" % a) for a in range(2)]
+        w1_raw = {}
+        w3_raw = {}
+        for a in range(2):
+            w1_raw[a, 0] = load_rows(w1[PASS * a : PASS * (a + 1), 0:BANK], "w1_raw")
+        pick2 = load_list(pos2, "pick2")
+        w3_raw[0] = load_rows(w3[:, 0:BANK], "w3_raw")
+        load_scale_rows([nc.sync] * 4, plane3, tab3_scales)
+        list3 = load_list(offs3, "list3")
+        words3 = load_words(tab3_words[0], "words3")
+        pick1 = load_list(pos1, "pick1")
+        keel_sb = keep([P, 2, PACK], F32, "keel_sb")
+        nc.sync.dma_start(out=keel_sb[:], in_=keel.rearrange("(b p t) -> p b t", b=2, t=PACK))
+        ask_sb = []
+        for b in range(2):
+            ask_sb.append(keep([P, PACK, J], F32, "ask%d" % b))
+        nc.sync.dma_start(out=ask_sb[0][:], in_=ask[0:PASS, :].rearrange("(p t) j -> p t j", t=PACK))
+        pick3 = load_list(pos3, "pick3")
+        for a in range(2):
+            w1_raw[a, 1] = load_rows(w1[PASS * a : PASS * (a + 1), BANK:H], "w1_raw")
+        w3_raw[1] = load_rows(w3[:, BANK:H], "w3_raw")
+        nc.sync.dma_start(out=ask_sb[1][:], in_=ask[PASS:H, :].rearrange("(p t) j -> p t j", t=PACK))
+        w4_sb = keep([P, 2, 2 * N], U8, "w4_sb")
+        nc.sync.dma_start(out=w4_sb[:].bitcast(I32), in_=w4_words.rearrange("a p c -> p a c").bitcast(I32))
+        for q in range(4):
+            nc.sync.dma_start(
+                out=w4_plane[32 * q : 32 * q + 4, :].rearrange("p (a c) -> p a c", a=2).bitcast(I32),
+                in_=w4_scales[:, 4 * q : 4 * q + 4, :].rearrange("a r c -> r a c").bitcast(I32),
+            )
+
+        neg_keel = keep([P, 2 * PACK], F32, "neg_keel")
+        nc.gpsimd.tensor_scalar(neg_keel[:], keel_sb[:].rearrange("p b t -> p (b t)"), -1.0, 0.0, ALU.mult, ALU.add)
+
+        def gather_plane(plane, offsets, name):
+            tile = keep([P, S], U8, name)
+            nc.vector.tensor_copy(tile[:], plane[:].indirect(offsets[:]))
+            return tile
+
+        def gather_words(words, offsets, name, pieces):
+            tile = keep([P, S], U32, name)
+            n = S // pieces
+            for u in range(pieces):
+                nc.vector.tensor_copy(
+                    tile[:, n * u : n * (u + 1)],
+                    words[:].bitcast(U32).indirect(offsets[:, n // 16 * u : n // 16 * (u + 1)]),
+                )
+            return tile
+
+        def quantise_weight(raw, name):
+            grouped = ring.tile([P, PACK * BANK], BF16, name="grouped", tag="grouped", bufs=3, align_bytes=64)
+            nc.scalar.copy(
+                out=grouped[:].rearrange("p (t m j) -> p m j t", t=PACK, j=PACK),
+                in_=raw[:].rearrange("p j (m t) -> p m j t", t=PACK),
+            )
+            codes = keep([P, BANK], U32, name + "_codes")
+            plane = keep([P, BANK], U8, name + "_plane")
+            nc.vector.quantize_mx(out=codes[:].bitcast(FP8X4), scales=plane[:], in_=grouped[:])
+            return codes, plane
+
+        def rows_tile(tag, bufs):
+            return ring.tile([P, S], F32, name=tag, tag=tag, bufs=bufs, align_bytes=64)
+
+        def first_stage(window, h, weights, t, operands, scale=None):
+            m = slice(P * t, P * (t + 1))
+            cols = slice(BANK * h, BANK * (h + 1))
+            acc = psum.tile([P, BANK], F32, name="acc", tag="acc")
+            for a, ((codes, plane), (words, words_plane)) in enumerate(zip(weights, operands)):
+                nc.tensor.matmul_mx(
+                    out=acc[:], lhsT=codes[:, m].bitcast(FP8X4), lhsT_scale=plane[:, m],
+                    rhs=words[:, cols].bitcast(FP8X4), rhs_scale=words_plane[PACK * a : P, cols],
+                    start=(a == 0), stop=(a == len(weights) - 1),
+                )
+            if scale is None:
+                nc.scalar.copy(out=window[:, cols], in_=acc[:])
+            else:
+                nc.scalar.activation(out=window[:, cols], in_=acc[:], func=ACT.Copy, scale=scale)
+
+        w2_q = []
+        for b in range(2):
+            cols = slice(BANK * b, BANK * (b + 1))
+            codes = keep([P, BANK], U32, "w2_codes%d" % b)
+            plane = keep([P, BANK], U8, "w2_plane%d" % b)
+            nc.scalar.copy(
+                out=codes[:].rearrange("p (t c i) -> p c t i", t=PACK, i=4),
+                in_=w2_raw[:, cols].bitcast(U32).rearrange("p (c i t) -> p c t i", t=PACK, i=4),
+            )
+            nc.gpsimd.tensor_copy(
+                out=plane[:].rearrange("p (t m) -> p t m", t=PACK),
+                in_=w2_plane_raw[:, cols].rearrange("p (m t) -> p t m", t=PACK),
+            )
+            w2_q.append((codes, plane))
+
+        v2_plane = gather_plane(plane2, list2, "v2_plane")
+        v2 = [(gather_words(words2, list2, "v2_words", 2), v2_plane)]
+
+        b_picked = {}
+
+        def berth(i):
+            window = rows_tile("b_rows", 5)
+            for h in range(2):
+                first_stage(window, h, [w2_q[i // PACK]], i % PACK, v2)
+            return window
+
+        def berth_pick(i, window):
+            b_picked[i] = ring.tile([P, J], F32, name="picked", tag="picked", bufs=8, align_bytes=64)
+            nc.vector.tensor_copy(b_picked[i][:], window[:].indirect(pick2[:]))
+
+        early = [berth(i) for i in range(2)]
+        v1_plane = gather_plane(plane1, list1, "v1_plane")
+        v1 = [(gather_words(words1[a], list1, "v1_words%d" % a, 1), v1_plane) for a in range(2)]
+        w1_q = {0: [quantise_weight(w1_raw[a, 0], "w1_%d0" % a) for a in range(2)]}
+        early.extend(berth(i) for i in range(2, 5))
+        v3_plane = gather_plane(plane3, list3, "v3_plane")
+        v3 = [(gather_words(words3, list3, "v3_words", 1), v3_plane)]
+        w3_q = {0: [quantise_weight(w3_raw[0], "w3_0")]}
+        for i in range(5):
+            berth_pick(i, early[i])
+
+        z_q = {}
+        z_rows = {}
+
+        def quantise_z(b, cols, engine, name):
+            width = cols.stop - cols.start
+            grouped = ring.tile([P, PACK * width], BF16, name="grouped", tag="grouped", bufs=3, align_bytes=64)
+            dst = grouped[:].rearrange("p (c i t) -> p c t i", t=PACK, i=4)
+            src = z_rows[b][:, :, cols].rearrange("p t (c i) -> p c t i", i=4)
+            if engine is nc.scalar:
+                nc.scalar.copy(out=dst, in_=src)
+            else:
+                nc.vector.tensor_copy(out=dst, in_=src)
+            codes = keep([P, width], U32, name + "_codes")
+            plane = keep([P, width], U8, name + "_plane")
+            nc.vector.quantize_mx(out=codes[:].bitcast(FP8X4), scales=plane[:], in_=grouped[:])
+            return codes, plane
+
+        def second_stage(h):
+            for q in range(2):
+                acc = psum.tile([P, 2, HALF], F32, name="y_acc", tag="y_acc")
+                for b in range(2):
+                    codes, plane = z_q[b, h]
+                    for u in range(2):
+                        n = 2 * q + u
+                        nc.tensor.matmul_mx(
+                            out=acc[:, u, :],
+                            lhsT=w4_sb[:, b, 2 * P * n : 2 * P * (n + 1)].bitcast(FP4X4),
+                            lhsT_scale=w4_plane[:, N * b + P * n : N * b + P * (n + 1)],
+                            rhs=codes.bitcast(FP8X4), rhs_scale=plane,
+                            start=(b == 0 and u == 0), stop=(b == 1 and u == 1),
+                        )
+                bent = ring.tile([P, 2, HALF], F32, name="bent", tag="fit", bufs=3, align_bytes=64)
+                nc.scalar.activation(out=bent[:], in_=acc[:], func=ACT.Tanh)
+                result = ring.tile([P, 2, HALF], F32, name="result", tag="picked", bufs=8, align_bytes=64)
+                nc.vector.tensor_tensor(result[:], acc[:], bent[:], ALU.add)
+                nc.sync.dma_start(
+                    out=out[2 * P * q : 2 * P * (q + 1), HALF * h : HALF * (h + 1)].rearrange("(u p) j -> p u j", u=2),
+                    in_=result[:],
+                )
+
+        fits = {}
+        tiles = 2 * PACK
+        for step in range(tiles + 1):
+            i, k = step, step - 1
+            if i < tiles:
+                a_rows = rows_tile("a_rows", 3)
+            if k >= 0:
+                d_rows = rows_tile("d_rows", 3)
+                if k % PACK == 0:
+                    z_rows[k // PACK] = ring.tile([P, PACK, J], F32, name="z_rows", tag="wide", bufs=5, align_bytes=64)
+            for h in range(2):
+                if i < tiles:
+                    first_stage(a_rows, h, w1_q[i // PACK], i % PACK, v1)
+                if k >= 0:
+                    first_stage(d_rows, h, w3_q[k // PACK], k % PACK, v3, scale=neg_keel[:, k : k + 1])
+            if i < tiles:
+                fits[i] = ring.tile([P, J], F32, name="fit", tag="fit", bufs=3, align_bytes=64)
+                nc.vector.tensor_tensor(fits[i][:], a_rows[:].indirect(pick1[:]), ask_sb[i // PACK][:, i % PACK, :], ALU.add)
+            if k >= 0:
+                for cols in ([slice(0, HALF), slice(HALF, J)] if k == tiles - 1 else [slice(0, J)]):
+                    entries = slice(cols.start // 16, cols.stop // 16)
+                    nc.vector.tensor_tensor(
+                        z_rows[k // PACK][:, k % PACK, cols], d_rows[:].indirect(pick3[:, entries]), fits[k][:, cols], ALU.add
+                    )
+            if i < tiles:
+                nc.vector.tensor_tensor(fits[i][:], fits[i][:], b_picked[i][:], ALU.min)
+            if i < 3:
+                berth_pick(i + 5, berth(i + 5))
+            if i == 1:
+                w1_q[1] = [quantise_weight(w1_raw[a, 1], "w1_%d1" % a) for a in range(2)]
+            if i == 2:
+                w3_q[1] = [quantise_weight(w3_raw[1], "w3_1")]
+            if k == PACK + 1:
+                codes, plane = quantise_z(0, slice(0, J), nc.scalar, "z0")
+                for h in range(2):
+                    z_q[0, h] = (codes[:, HALF * h : HALF * (h + 1)], plane[:, HALF * h : HALF * (h + 1)])
+        for h in range(2):
+            codes, plane = quantise_z(1, slice(HALF * h, HALF * (h + 1)), nc.scalar if h == 0 else nc.vector, "z1%d" % h)
+            z_q[1, h] = (codes[:], plane[:])
+        for h in range(2):
+            second_stage(h)

@@ -47,10 +47,10 @@ def tile_list_berth_tide_features_kernel(
             engine.memset(tile[:].bitcast(I32), 0)
             return tile
 
-        def load_scale_rows(queues, plane, scales):
+        def load_scale_rows(plane, scales):
             rows = PACK * scales.shape[0]
-            for q, queue in enumerate(queues):
-                queue.dma_start(
+            for q in range(4):
+                nc.sync.dma_start(
                     out=plane[32 * q : 32 * q + rows, :].bitcast(I32),
                     in_=scales[:, 4 * q : 4 * q + 4, :].bitcast(I32),
                 )
@@ -73,19 +73,22 @@ def tile_list_berth_tide_features_kernel(
 
         list2 = load_list(offs2, "list2")
         list1 = load_list(offs, "list1")
-        load_scale_rows([nc.sync] * 4, plane2, tab2_scales)
+        load_scale_rows(plane2, tab2_scales)
         words2 = load_words(tab2_words[0], "words2")
         w2_raw = load_words(w2_words[0], "w2_raw")
-        load_scale_rows([nc.gpsimd] * 3 + [nc.sync], w2_plane_raw, w2_scales)
-        load_scale_rows([nc.sync] * 4, plane1, tab_scales)
-        words1 = [load_words(tab_words[a], "words1_%d" % a) for a in range(2)]
+        load_scale_rows(w2_plane_raw, w2_scales)
+        words1 = [load_words(tab_words[0], "words1_0")]
+        load_scale_rows(plane1, tab_scales)
+        words1.append(load_words(tab_words[1], "words1_1"))
         w1_raw = {}
         w3_raw = {}
         for a in range(2):
             w1_raw[a, 0] = load_rows(w1[PASS * a : PASS * (a + 1), 0:BANK], "w1_raw")
         pick2 = load_list(pos2, "pick2")
         w3_raw[0] = load_rows(w3[:, 0:BANK], "w3_raw")
-        load_scale_rows([nc.sync] * 4, plane3, tab3_scales)
+        for a in range(2):
+            w1_raw[a, 1] = load_rows(w1[PASS * a : PASS * (a + 1), BANK:H], "w1_raw")
+        load_scale_rows(plane3, tab3_scales)
         list3 = load_list(offs3, "list3")
         words3 = load_words(tab3_words[0], "words3")
         pick1 = load_list(pos1, "pick1")
@@ -96,8 +99,6 @@ def tile_list_berth_tide_features_kernel(
             ask_sb.append(keep([P, PACK, J], F32, "ask%d" % b))
         nc.sync.dma_start(out=ask_sb[0][:], in_=ask[0:PASS, :].rearrange("(p t) j -> p t j", t=PACK))
         pick3 = load_list(pos3, "pick3")
-        for a in range(2):
-            w1_raw[a, 1] = load_rows(w1[PASS * a : PASS * (a + 1), BANK:H], "w1_raw")
         w3_raw[1] = load_rows(w3[:, BANK:H], "w3_raw")
         nc.sync.dma_start(out=ask_sb[1][:], in_=ask[PASS:H, :].rearrange("(p t) j -> p t j", t=PACK))
         w4_sb = keep([P, 2, 2 * N], U8, "w4_sb")
@@ -164,7 +165,7 @@ def tile_list_berth_tide_features_kernel(
                 out=codes[:].rearrange("p (t c i) -> p c t i", t=PACK, i=4),
                 in_=w2_raw[:, cols].bitcast(U32).rearrange("p (c i t) -> p c t i", t=PACK, i=4),
             )
-            nc.gpsimd.tensor_copy(
+            nc.vector.tensor_copy(
                 out=plane[:].rearrange("p (t m) -> p t m", t=PACK),
                 in_=w2_plane_raw[:, cols].rearrange("p (m t) -> p t m", t=PACK),
             )
@@ -176,25 +177,23 @@ def tile_list_berth_tide_features_kernel(
         b_picked = {}
 
         def berth(i):
-            window = rows_tile("b_rows", 5)
+            window = rows_tile("b_rows", 3)
             for h in range(2):
                 first_stage(window, h, [w2_q[i // PACK]], i % PACK, v2)
-            return window
-
-        def berth_pick(i, window):
             b_picked[i] = ring.tile([P, J], F32, name="picked", tag="picked", bufs=8, align_bytes=64)
             nc.vector.tensor_copy(b_picked[i][:], window[:].indirect(pick2[:]))
 
-        early = [berth(i) for i in range(2)]
         v1_plane = gather_plane(plane1, list1, "v1_plane")
         v1 = [(gather_words(words1[a], list1, "v1_words%d" % a, 1), v1_plane) for a in range(2)]
         w1_q = {0: [quantise_weight(w1_raw[a, 0], "w1_%d0" % a) for a in range(2)]}
-        early.extend(berth(i) for i in range(2, 5))
+        for i in range(6):
+            berth(i)
+        w3_q = {0: [quantise_weight(w3_raw[0], "w3_0")]}
+        for i in range(6, 8):
+            berth(i)
+        w1_q[1] = [quantise_weight(w1_raw[a, 1], "w1_%d1" % a) for a in range(2)]
         v3_plane = gather_plane(plane3, list3, "v3_plane")
         v3 = [(gather_words(words3, list3, "v3_words", 1), v3_plane)]
-        w3_q = {0: [quantise_weight(w3_raw[0], "w3_0")]}
-        for i in range(5):
-            berth_pick(i, early[i])
 
         z_q = {}
         z_rows = {}
@@ -236,44 +235,57 @@ def tile_list_berth_tide_features_kernel(
                     in_=result[:],
                 )
 
+        def pick_a(i, a_rows, fit, cols):
+            entries = slice(cols.start // 16, cols.stop // 16)
+            nc.vector.tensor_tensor(fit, a_rows[:].indirect(pick1[:, entries]), ask_sb[i // PACK][:, i % PACK, cols], ALU.add)
+
+        def smaller(i, fit, cols):
+            nc.vector.tensor_tensor(fit, fit, b_picked[i][:, cols], ALU.min)
+
+        def pick_d(i, d_rows, fit, cols):
+            entries = slice(cols.start // 16, cols.stop // 16)
+            nc.vector.tensor_tensor(z_rows[i // PACK][:, i % PACK, cols], d_rows[:].indirect(pick3[:, entries]), fit, ALU.add)
+
         fits = {}
+        a_rows = {}
+        d_rows = {}
         tiles = 2 * PACK
+        whole = tiles - 2
+        every = slice(0, J)
         for step in range(tiles + 1):
             i, k = step, step - 1
             if i < tiles:
-                a_rows = rows_tile("a_rows", 3)
+                a_rows[i] = rows_tile("a_rows", 4)
             if k >= 0:
-                d_rows = rows_tile("d_rows", 3)
+                d_rows[k] = rows_tile("d_rows", 4)
                 if k % PACK == 0:
                     z_rows[k // PACK] = ring.tile([P, PACK, J], F32, name="z_rows", tag="wide", bufs=5, align_bytes=64)
             for h in range(2):
                 if i < tiles:
-                    first_stage(a_rows, h, w1_q[i // PACK], i % PACK, v1)
+                    first_stage(a_rows[i], h, w1_q[i // PACK], i % PACK, v1)
                 if k >= 0:
-                    first_stage(d_rows, h, w3_q[k // PACK], k % PACK, v3, scale=neg_keel[:, k : k + 1])
-            if i < tiles:
+                    first_stage(d_rows[k], h, w3_q[k // PACK], k % PACK, v3, scale=neg_keel[:, k : k + 1])
+            if i < whole:
                 fits[i] = ring.tile([P, J], F32, name="fit", tag="fit", bufs=3, align_bytes=64)
-                nc.vector.tensor_tensor(fits[i][:], a_rows[:].indirect(pick1[:]), ask_sb[i // PACK][:, i % PACK, :], ALU.add)
-            if k >= 0:
-                for cols in ([slice(0, HALF), slice(HALF, J)] if k == tiles - 1 else [slice(0, J)]):
-                    entries = slice(cols.start // 16, cols.stop // 16)
-                    nc.vector.tensor_tensor(
-                        z_rows[k // PACK][:, k % PACK, cols], d_rows[:].indirect(pick3[:, entries]), fits[k][:, cols], ALU.add
-                    )
-            if i < tiles:
-                nc.vector.tensor_tensor(fits[i][:], fits[i][:], b_picked[i][:], ALU.min)
-            if i < 3:
-                berth_pick(i + 5, berth(i + 5))
-            if i == 1:
-                w1_q[1] = [quantise_weight(w1_raw[a, 1], "w1_%d1" % a) for a in range(2)]
+                pick_a(i, a_rows[i], fits[i][:], every)
+            if 0 <= k < whole:
+                pick_d(k, d_rows[k], fits[k][:], every)
+            if i < whole:
+                smaller(i, fits[i][:], every)
             if i == 2:
                 w3_q[1] = [quantise_weight(w3_raw[1], "w3_1")]
-            if k == PACK + 1:
-                codes, plane = quantise_z(0, slice(0, J), nc.scalar, "z0")
-                for h in range(2):
-                    z_q[0, h] = (codes[:, HALF * h : HALF * (h + 1)], plane[:, HALF * h : HALF * (h + 1)])
+        codes, plane = quantise_z(0, every, nc.scalar, "z0")
         for h in range(2):
-            codes, plane = quantise_z(1, slice(HALF * h, HALF * (h + 1)), nc.scalar if h == 0 else nc.vector, "z1%d" % h)
+            z_q[0, h] = (codes[:, HALF * h : HALF * (h + 1)], plane[:, HALF * h : HALF * (h + 1)])
+        for h in range(2):
+            cols = slice(HALF * h, HALF * (h + 1))
+            pair = ring.tile([P, 2, HALF], F32, name="pair", tag="pair", bufs=1, align_bytes=64)
+            for u in range(2):
+                pick_a(whole + u, a_rows[whole + u], pair[:, u, :], cols)
+            for u in range(2):
+                smaller(whole + u, pair[:, u, :], cols)
+            for u in range(2):
+                pick_d(whole + u, d_rows[whole + u], pair[:, u, :], cols)
+            codes, plane = quantise_z(1, cols, nc.scalar if h == 0 else nc.vector, "z1%d" % h)
             z_q[1, h] = (codes[:], plane[:])
-        for h in range(2):
             second_stage(h)

@@ -55,6 +55,10 @@ def tile_list_berth_tide_features_kernel(
                     in_=scales[:, 4 * q : 4 * q + 4, :].bitcast(I32),
                 )
 
+        def load_spread_rows(plane, rows):
+            for r in range(4):
+                nc.sync.dma_start(out=plane[r:P:32].bitcast(I32), in_=rows[r:16:4].bitcast(I32))
+
         def load_words(words, name):
             tile = keep([P, words.shape[1]], I32, name)
             nc.sync.dma_start(out=tile[:], in_=words.rearrange("p c i -> p (c i)").bitcast(I32))
@@ -73,10 +77,10 @@ def tile_list_berth_tide_features_kernel(
 
         list2 = load_list(offs2, "list2")
         list1 = load_list(offs, "list1")
-        load_scale_rows(plane2, tab2_scales)
+        load_spread_rows(plane2[:], tab2_scales[0])
         words2 = load_words(tab2_words[0], "words2")
         w2_raw = load_words(w2_words[0], "w2_raw")
-        load_scale_rows(w2_plane_raw, w2_scales)
+        load_spread_rows(w2_plane_raw[:], w2_scales[0])
         words1 = [load_words(tab_words[0], "words1_0")]
         load_scale_rows(plane1, tab_scales)
         words1.append(load_words(tab_words[1], "words1_1"))
@@ -88,7 +92,7 @@ def tile_list_berth_tide_features_kernel(
         w3_raw[0] = load_rows(w3[:, 0:BANK], "w3_raw")
         for a in range(2):
             w1_raw[a, 1] = load_rows(w1[PASS * a : PASS * (a + 1), BANK:H], "w1_raw")
-        load_scale_rows(plane3, tab3_scales)
+        load_spread_rows(plane3[:], tab3_scales[0])
         list3 = load_list(offs3, "list3")
         words3 = load_words(tab3_words[0], "words3")
         pick1 = load_list(pos1, "pick1")
@@ -103,11 +107,7 @@ def tile_list_berth_tide_features_kernel(
         nc.sync.dma_start(out=ask_sb[1][:], in_=ask[PASS:H, :].rearrange("(p t) j -> p t j", t=PACK))
         w4_sb = keep([P, 2, 2 * N], U8, "w4_sb")
         nc.sync.dma_start(out=w4_sb[:].bitcast(I32), in_=w4_words.rearrange("a p c -> p a c").bitcast(I32))
-        for q in range(4):
-            nc.sync.dma_start(
-                out=w4_plane[32 * q : 32 * q + 4, :].rearrange("p (a c) -> p a c", a=2).bitcast(I32),
-                in_=w4_scales[:, 4 * q : 4 * q + 4, :].rearrange("a r c -> r a c").bitcast(I32),
-            )
+        load_spread_rows(w4_plane[:].rearrange("p (a c) -> p a c", a=2), w4_scales.rearrange("a q c -> q a c"))
 
         neg_keel = keep([P, 2 * PACK], F32, "neg_keel")
         nc.gpsimd.tensor_scalar(neg_keel[:], keel_sb[:].rearrange("p b t -> p (b t)"), -1.0, 0.0, ALU.mult, ALU.add)

@@ -21,6 +21,18 @@ PACK = 4
 PASS = P * PACK
 BANK = 512
 HALF = J // 2
+PER_COLUMN = 16
+LINE = 4
+TILES = H // P
+WHOLE_TILES = TILES - 2
+
+WIDE_BUFS = 5
+GROUPED_BUFS = 3
+A_BUFS, B_BUFS, D_BUFS = 3, 6, 4
+PICKED_BUFS = TILES
+FIT_BUFS = 3
+ACC_BUFS = 4
+W3_LATE_STEP = 2
 
 
 def tile_list_berth_tide_features_kernel(
@@ -32,260 +44,255 @@ def tile_list_berth_tide_features_kernel(
     with ExitStack() as ctx:
         held = ctx.enter_context(tc.tile_pool(name="held", bufs=1))
         ring = ctx.enter_context(tc.tile_pool(name="ring", bufs=1))
-        psum = ctx.enter_context(tc.psum_pool(name="psum", bufs=4))
+        psum = ctx.enter_context(tc.psum_pool(name="psum", bufs=ACC_BUFS))
 
         def keep(shape, dtype, name):
             return held.tile(shape, dtype, name=name, align_bytes=64)
+
+        def rotate(shape, dtype, name, tag, bufs):
+            return ring.tile(shape, dtype, name=name, tag=tag, bufs=bufs, align_bytes=64)
 
         def load_list(src, name):
             tile = held.tile(list(src.shape), U16, name=name)
             nc.sync.dma_start(tile[:], src)
             return tile
 
+        def entries(offsets, cols):
+            return offsets[:, cols.start // PER_COLUMN : cols.stop // PER_COLUMN]
+
         def zeroed_plane(engine, width, name):
             tile = keep([P, width], U8, name)
             engine.memset(tile[:].bitcast(I32), 0)
             return tile
 
-        def load_scale_rows(plane, scales):
-            rows = PACK * scales.shape[0]
-            for q in range(4):
-                nc.sync.dma_start(
-                    out=plane[32 * q : 32 * q + rows, :].bitcast(I32),
-                    in_=scales[:, 4 * q : 4 * q + 4, :].bitcast(I32),
-                )
-
-        def load_spread_rows(plane, rows):
+        def load_plane(plane, rows):
             for r in range(4):
                 nc.sync.dma_start(out=plane[r:P:32].bitcast(I32), in_=rows[r:16:4].bitcast(I32))
+
+        def load_two_planes(plane, scales):
+            for q in range(4):
+                nc.sync.dma_start(
+                    out=plane[32 * q : 32 * q + 8, :].bitcast(I32),
+                    in_=scales[:, 4 * q : 4 * q + 4, :].bitcast(I32),
+                )
 
         def load_words(words, name):
             tile = keep([P, words.shape[1]], I32, name)
             nc.sync.dma_start(out=tile[:], in_=words.rearrange("p c i -> p (c i)").bitcast(I32))
             return tile
 
-        def load_rows(rows, name):
-            tile = ring.tile([P, PACK, BANK], F32, name=name, tag="wide", bufs=5, align_bytes=64)
-            nc.sync.dma_start(out=tile[:], in_=rows.rearrange("(p j) c -> p j c", j=PACK))
+        def load_weight(rows, name):
+            tile = rotate([P, PACK, BANK], F32, name, "wide", WIDE_BUFS)
+            nc.sync.dma_start(out=tile[:], in_=rows.rearrange("(p i) c -> p i c", i=PACK))
             return tile
 
-        plane2 = zeroed_plane(nc.gpsimd, T, "plane2")
+        def load_ask(g):
+            rows = ask[PASS * g : PASS * (g + 1), :]
+            nc.sync.dma_start(out=ask_sb[g][:], in_=rows.rearrange("(p t) j -> p t j", t=PACK))
+
+        tab2_plane = zeroed_plane(nc.gpsimd, T, "tab2_plane")
         w2_plane_raw = zeroed_plane(nc.gpsimd, H, "w2_plane_raw")
-        plane1 = zeroed_plane(nc.vector, T, "plane1")
-        plane3 = zeroed_plane(nc.vector, T, "plane3")
+        tab_plane = zeroed_plane(nc.vector, T, "tab_plane")
+        tab3_plane = zeroed_plane(nc.vector, T, "tab3_plane")
         w4_plane = zeroed_plane(nc.vector, 2 * N, "w4_plane")
 
-        list2 = load_list(offs2, "list2")
-        list1 = load_list(offs, "list1")
-        load_spread_rows(plane2[:], tab2_scales[0])
-        words2 = load_words(tab2_words[0], "words2")
+        idx2 = load_list(offs2, "idx2")
+        idx = load_list(offs, "idx")
+        load_plane(tab2_plane[:], tab2_scales[0])
+        tab2_sb = load_words(tab2_words[0], "tab2_sb")
+        tab_sb = [load_words(tab_words[0], "tab_sb0")]
+        load_plane(w2_plane_raw[:], w2_scales[0])
         w2_raw = load_words(w2_words[0], "w2_raw")
-        load_spread_rows(w2_plane_raw[:], w2_scales[0])
-        words1 = [load_words(tab_words[0], "words1_0")]
-        load_scale_rows(plane1, tab_scales)
-        words1.append(load_words(tab_words[1], "words1_1"))
-        w1_raw = {}
-        w3_raw = {}
-        for a in range(2):
-            w1_raw[a, 0] = load_rows(w1[PASS * a : PASS * (a + 1), 0:BANK], "w1_raw")
-        pick2 = load_list(pos2, "pick2")
-        w3_raw[0] = load_rows(w3[:, 0:BANK], "w3_raw")
-        for a in range(2):
-            w1_raw[a, 1] = load_rows(w1[PASS * a : PASS * (a + 1), BANK:H], "w1_raw")
-        load_spread_rows(plane3[:], tab3_scales[0])
-        list3 = load_list(offs3, "list3")
-        words3 = load_words(tab3_words[0], "words3")
-        pick1 = load_list(pos1, "pick1")
+        load_two_planes(tab_plane, tab_scales)
+        tab_sb.append(load_words(tab_words[1], "tab_sb1"))
+        p2 = load_list(pos2, "p2")
+        w1_raw = {0: [load_weight(w1[PASS * c : PASS * (c + 1), 0:BANK], "w1_raw") for c in range(2)]}
+        load_plane(tab3_plane[:], tab3_scales[0])
+        idx3 = load_list(offs3, "idx3")
+        w3_raw = {0: load_weight(w3[:, 0:BANK], "w3_raw")}
+        w1_raw[1] = [load_weight(w1[PASS * c : PASS * (c + 1), BANK:H], "w1_raw") for c in range(2)]
+        tab3_sb = load_words(tab3_words[0], "tab3_sb")
+        p1 = load_list(pos1, "p1")
         keel_sb = keep([P, 2, PACK], F32, "keel_sb")
-        nc.sync.dma_start(out=keel_sb[:], in_=keel.rearrange("(b p t) -> p b t", b=2, t=PACK))
-        ask_sb = []
-        for b in range(2):
-            ask_sb.append(keep([P, PACK, J], F32, "ask%d" % b))
-        nc.sync.dma_start(out=ask_sb[0][:], in_=ask[0:PASS, :].rearrange("(p t) j -> p t j", t=PACK))
-        pick3 = load_list(pos3, "pick3")
-        w3_raw[1] = load_rows(w3[:, BANK:H], "w3_raw")
-        nc.sync.dma_start(out=ask_sb[1][:], in_=ask[PASS:H, :].rearrange("(p t) j -> p t j", t=PACK))
+        nc.sync.dma_start(out=keel_sb[:], in_=keel.rearrange("(g p t) -> p g t", g=2, t=PACK))
+        ask_sb = [keep([P, PACK, J], F32, "ask_sb%d" % g) for g in range(2)]
+        load_ask(0)
+        p3 = load_list(pos3, "p3")
+        w3_raw[1] = load_weight(w3[:, BANK:H], "w3_raw")
+        load_ask(1)
         w4_sb = keep([P, 2, 2 * N], U8, "w4_sb")
-        nc.sync.dma_start(out=w4_sb[:].bitcast(I32), in_=w4_words.rearrange("a p c -> p a c").bitcast(I32))
-        load_spread_rows(w4_plane[:].rearrange("p (a c) -> p a c", a=2), w4_scales.rearrange("a q c -> q a c"))
+        nc.sync.dma_start(out=w4_sb[:].bitcast(I32), in_=w4_words.rearrange("g p c -> p g c").bitcast(I32))
+        load_plane(w4_plane[:].rearrange("p (g c) -> p g c", g=2), w4_scales.rearrange("g q c -> q g c"))
 
-        neg_keel = keep([P, 2 * PACK], F32, "neg_keel")
-        nc.gpsimd.tensor_scalar(neg_keel[:], keel_sb[:].rearrange("p b t -> p (b t)"), -1.0, 0.0, ALU.mult, ALU.add)
+        neg_keel = keep([P, TILES], F32, "neg_keel")
+        nc.gpsimd.tensor_scalar(neg_keel[:], keel_sb[:].rearrange("p g t -> p (g t)"), -1.0, 0.0, ALU.mult, ALU.add)
 
         def gather_plane(plane, offsets, name):
             tile = keep([P, S], U8, name)
             nc.vector.tensor_copy(tile[:], plane[:].indirect(offsets[:]))
             return tile
 
-        def gather_words(words, offsets, name, pieces):
+        def gather_words(words, offsets, name, width):
             tile = keep([P, S], U32, name)
-            n = S // pieces
-            for u in range(pieces):
-                nc.vector.tensor_copy(
-                    tile[:, n * u : n * (u + 1)],
-                    words[:].bitcast(U32).indirect(offsets[:, n // 16 * u : n // 16 * (u + 1)]),
-                )
+            for start in range(0, S, width):
+                cols = slice(start, start + width)
+                nc.vector.tensor_copy(tile[:, cols], words[:].bitcast(U32).indirect(entries(offsets, cols)))
             return tile
 
-        def quantise_weight(raw, name):
-            grouped = ring.tile([P, PACK * BANK], BF16, name="grouped", tag="grouped", bufs=3, align_bytes=64)
-            nc.scalar.copy(
-                out=grouped[:].rearrange("p (t m j) -> p m j t", t=PACK, j=PACK),
-                in_=raw[:].rearrange("p j (m t) -> p m j t", t=PACK),
-            )
-            codes = keep([P, BANK], U32, name + "_codes")
-            plane = keep([P, BANK], U8, name + "_plane")
-            nc.vector.quantize_mx(out=codes[:].bitcast(FP8X4), scales=plane[:], in_=grouped[:])
-            return codes, plane
-
-        def rows_tile(tag, bufs):
-            return ring.tile([P, S], F32, name=tag, tag=tag, bufs=bufs, align_bytes=64)
-
-        def first_stage(window, h, weights, t, operands, scale=None):
-            m = slice(P * t, P * (t + 1))
-            cols = slice(BANK * h, BANK * (h + 1))
-            acc = psum.tile([P, BANK], F32, name="acc", tag="acc")
-            for a, ((codes, plane), (words, words_plane)) in enumerate(zip(weights, operands)):
-                nc.tensor.matmul_mx(
-                    out=acc[:], lhsT=codes[:, m].bitcast(FP8X4), lhsT_scale=plane[:, m],
-                    rhs=words[:, cols].bitcast(FP8X4), rhs_scale=words_plane[PACK * a : P, cols],
-                    start=(a == 0), stop=(a == len(weights) - 1),
-                )
-            if scale is None:
-                nc.scalar.copy(out=window[:, cols], in_=acc[:])
-            else:
-                nc.scalar.activation(out=window[:, cols], in_=acc[:], func=ACT.Copy, scale=scale)
-
-        w2_q = []
-        for b in range(2):
-            cols = slice(BANK * b, BANK * (b + 1))
-            codes = keep([P, BANK], U32, "w2_codes%d" % b)
-            plane = keep([P, BANK], U8, "w2_plane%d" % b)
-            nc.scalar.copy(
-                out=codes[:].rearrange("p (t c i) -> p c t i", t=PACK, i=4),
-                in_=w2_raw[:, cols].bitcast(U32).rearrange("p (c i t) -> p c t i", t=PACK, i=4),
-            )
-            nc.vector.tensor_copy(
-                out=plane[:].rearrange("p (t m) -> p t m", t=PACK),
-                in_=w2_plane_raw[:, cols].rearrange("p (m t) -> p t m", t=PACK),
-            )
-            w2_q.append((codes, plane))
-
-        v2_plane = gather_plane(plane2, list2, "v2_plane")
-        v2 = [(gather_words(words2, list2, "v2_words", 2), v2_plane)]
-
-        b_picked = {}
-
-        def berth(i):
-            window = rows_tile("b_rows", 3)
-            for h in range(2):
-                first_stage(window, h, [w2_q[i // PACK]], i % PACK, v2)
-            b_picked[i] = ring.tile([P, J], F32, name="picked", tag="picked", bufs=8, align_bytes=64)
-            nc.vector.tensor_copy(b_picked[i][:], window[:].indirect(pick2[:]))
-
-        v1_plane = gather_plane(plane1, list1, "v1_plane")
-        v1 = [(gather_words(words1[a], list1, "v1_words%d" % a, 1), v1_plane) for a in range(2)]
-        w1_q = {0: [quantise_weight(w1_raw[a, 0], "w1_%d0" % a) for a in range(2)]}
-        for i in range(6):
-            berth(i)
-        w3_q = {0: [quantise_weight(w3_raw[0], "w3_0")]}
-        for i in range(6, 8):
-            berth(i)
-        w1_q[1] = [quantise_weight(w1_raw[a, 1], "w1_%d1" % a) for a in range(2)]
-        v3_plane = gather_plane(plane3, list3, "v3_plane")
-        v3 = [(gather_words(words3, list3, "v3_words", 1), v3_plane)]
-
-        z_q = {}
-        z_rows = {}
-
-        def quantise_z(b, cols, engine, name):
-            width = cols.stop - cols.start
-            grouped = ring.tile([P, PACK * width], BF16, name="grouped", tag="grouped", bufs=3, align_bytes=64)
-            dst = grouped[:].rearrange("p (c i t) -> p c t i", t=PACK, i=4)
-            src = z_rows[b][:, :, cols].rearrange("p t (c i) -> p c t i", i=4)
-            if engine is nc.scalar:
-                nc.scalar.copy(out=dst, in_=src)
-            else:
-                nc.vector.tensor_copy(out=dst, in_=src)
+        def quantise(grouped, width, name):
             codes = keep([P, width], U32, name + "_codes")
             plane = keep([P, width], U8, name + "_plane")
             nc.vector.quantize_mx(out=codes[:].bitcast(FP8X4), scales=plane[:], in_=grouped[:])
             return codes, plane
 
-        def second_stage(h):
-            for q in range(2):
+        def quantise_weight(raw, name):
+            grouped = rotate([P, PACK * BANK], BF16, "grouped", "grouped", GROUPED_BUFS)
+            nc.scalar.copy(
+                out=grouped[:].rearrange("p (t m i) -> p m i t", t=PACK, i=PACK),
+                in_=raw[:].rearrange("p i (m t) -> p m i t", t=PACK),
+            )
+            return quantise(grouped, BANK, name)
+
+        def first_stage(rows, bank, weight, t, looked_up, scale=None):
+            stationary = slice(P * t, P * (t + 1))
+            cols = slice(BANK * bank, BANK * (bank + 1))
+            acc = psum.tile([P, BANK], F32, name="acc", tag="acc")
+            for c, ((codes, plane), (words, words_plane)) in enumerate(zip(weight, looked_up)):
+                nc.tensor.matmul_mx(
+                    out=acc[:], lhsT=codes[:, stationary].bitcast(FP8X4), lhsT_scale=plane[:, stationary],
+                    rhs=words[:, cols].bitcast(FP8X4), rhs_scale=words_plane[4 * c : P, cols],
+                    start=(c == 0), stop=(c == len(weight) - 1),
+                )
+            if scale is None:
+                nc.scalar.copy(out=rows[:, cols], in_=acc[:])
+            else:
+                nc.scalar.activation(out=rows[:, cols], in_=acc[:], func=ACT.Copy, scale=scale)
+
+        w2_q = []
+        for g in range(2):
+            cols = slice(BANK * g, BANK * (g + 1))
+            codes = keep([P, BANK], U32, "w2_codes%d" % g)
+            plane = keep([P, BANK], U8, "w2_plane%d" % g)
+            nc.scalar.copy(
+                out=codes[:].rearrange("p (t u v) -> p u t v", t=PACK, v=LINE),
+                in_=w2_raw[:, cols].bitcast(U32).rearrange("p (u v t) -> p u t v", t=PACK, v=LINE),
+            )
+            nc.gpsimd.tensor_copy(
+                out=plane[:].rearrange("p (t m) -> p t m", t=PACK),
+                in_=w2_plane_raw[:, cols].rearrange("p (m t) -> p t m", t=PACK),
+            )
+            w2_q.append([(codes, plane)])
+
+        v2_plane = gather_plane(tab2_plane, idx2, "v2_plane")
+        v2 = [(gather_words(tab2_sb, idx2, "v2_words", BANK), v2_plane)]
+
+        b_picked = {}
+
+        def make_and_pick_b(i):
+            rows = rotate([P, S], F32, "b_rows", "b_rows", B_BUFS)
+            for bank in range(S // BANK):
+                first_stage(rows, bank, w2_q[i // PACK], i % PACK, v2)
+            b_picked[i] = rotate([P, J], F32, "picked", "picked", PICKED_BUFS)
+            nc.vector.tensor_copy(b_picked[i][:], rows[:].indirect(p2[:]))
+
+        v_plane = gather_plane(tab_plane, idx, "v_plane")
+        v = [(gather_words(tab_sb[c], idx, "v_words%d" % c, S), v_plane) for c in range(2)]
+        w1_q = {0: [quantise_weight(w1_raw[0][c], "w1_0%d" % c) for c in range(2)]}
+        for i in range(B_BUFS):
+            make_and_pick_b(i)
+        w3_q = {0: [quantise_weight(w3_raw[0], "w3_0")]}
+        for i in range(B_BUFS, TILES):
+            make_and_pick_b(i)
+        w1_q[1] = [quantise_weight(w1_raw[1][c], "w1_1%d" % c) for c in range(2)]
+        v3_plane = gather_plane(tab3_plane, idx3, "v3_plane")
+        v3 = [(gather_words(tab3_sb, idx3, "v3_words", S), v3_plane)]
+
+        z_rows = {}
+        z_q = {}
+
+        def quantise_z(g, cols, copy, name):
+            width = cols.stop - cols.start
+            grouped = rotate([P, PACK * width], BF16, "grouped", "grouped", GROUPED_BUFS)
+            copy(
+                out=grouped[:].rearrange("p (u v t) -> p u t v", t=PACK, v=LINE),
+                in_=z_rows[g][:, :, cols].rearrange("p t (u v) -> p u t v", v=LINE),
+            )
+            return quantise(grouped, width, name)
+
+        def second_stage(half):
+            for pair_of_tiles in range(N // (2 * P)):
                 acc = psum.tile([P, 2, HALF], F32, name="y_acc", tag="y_acc")
-                for b in range(2):
-                    codes, plane = z_q[b, h]
+                for g in range(2):
+                    codes, plane = z_q[g, half]
                     for u in range(2):
-                        n = 2 * q + u
+                        n = 2 * pair_of_tiles + u
                         nc.tensor.matmul_mx(
                             out=acc[:, u, :],
-                            lhsT=w4_sb[:, b, 2 * P * n : 2 * P * (n + 1)].bitcast(FP4X4),
-                            lhsT_scale=w4_plane[:, N * b + P * n : N * b + P * (n + 1)],
+                            lhsT=w4_sb[:, g, 2 * P * n : 2 * P * (n + 1)].bitcast(FP4X4),
+                            lhsT_scale=w4_plane[:, N * g + P * n : N * g + P * (n + 1)],
                             rhs=codes.bitcast(FP8X4), rhs_scale=plane,
-                            start=(b == 0 and u == 0), stop=(b == 1 and u == 1),
+                            start=(g == 0 and u == 0), stop=(g == 1 and u == 1),
                         )
-                bent = ring.tile([P, 2, HALF], F32, name="bent", tag="fit", bufs=3, align_bytes=64)
-                nc.scalar.activation(out=bent[:], in_=acc[:], func=ACT.Tanh)
-                result = ring.tile([P, 2, HALF], F32, name="result", tag="picked", bufs=8, align_bytes=64)
-                nc.vector.tensor_tensor(result[:], acc[:], bent[:], ALU.add)
-                nc.sync.dma_start(
-                    out=out[2 * P * q : 2 * P * (q + 1), HALF * h : HALF * (h + 1)].rearrange("(u p) j -> p u j", u=2),
-                    in_=result[:],
-                )
+                tanh_y = rotate([P, 2, HALF], F32, "tanh_y", "fit", FIT_BUFS)
+                nc.scalar.activation(out=tanh_y[:], in_=acc[:], func=ACT.Tanh)
+                result = rotate([P, 2, HALF], F32, "result", "picked", PICKED_BUFS)
+                nc.vector.tensor_tensor(result[:], acc[:], tanh_y[:], ALU.add)
+                rows = out[2 * P * pair_of_tiles : 2 * P * (pair_of_tiles + 1), HALF * half : HALF * (half + 1)]
+                nc.sync.dma_start(out=rows.rearrange("(u p) j -> p u j", u=2), in_=result[:])
 
-        def pick_a(i, a_rows, fit, cols):
-            entries = slice(cols.start // 16, cols.stop // 16)
-            nc.vector.tensor_tensor(fit, a_rows[:].indirect(pick1[:, entries]), ask_sb[i // PACK][:, i % PACK, cols], ALU.add)
-
-        def smaller(i, fit, cols):
-            nc.vector.tensor_tensor(fit, fit, b_picked[i][:, cols], ALU.min)
-
-        def pick_d(i, d_rows, fit, cols):
-            entries = slice(cols.start // 16, cols.stop // 16)
-            nc.vector.tensor_tensor(z_rows[i // PACK][:, i % PACK, cols], d_rows[:].indirect(pick3[:, entries]), fit, ALU.add)
-
-        fits = {}
         a_rows = {}
         d_rows = {}
-        tiles = 2 * PACK
-        whole = tiles - 2
+
+        def pick_a(i, fit, cols):
+            window = a_rows[i][:].indirect(entries(p1, cols))
+            nc.vector.tensor_tensor(fit, window, ask_sb[i // PACK][:, i % PACK, cols], ALU.add)
+
+        def take_min(i, fit, cols):
+            nc.vector.tensor_tensor(fit, fit, b_picked[i][:, cols], ALU.min)
+
+        def pick_d(i, fit, cols):
+            window = d_rows[i][:].indirect(entries(p3, cols))
+            nc.vector.tensor_tensor(z_rows[i // PACK][:, i % PACK, cols], window, fit, ALU.add)
+
+        in_turn = [("a", 0), ("d", 0), ("a", 1), ("d", 1)]
+        a_first = [("a", 0), ("a", 1), ("d", 0), ("d", 1)]
+        fits = {}
         every = slice(0, J)
-        for step in range(tiles + 1):
-            i, k = step, step - 1
-            if i < tiles:
-                a_rows[i] = rows_tile("a_rows", 4)
-            if k >= 0:
-                d_rows[k] = rows_tile("d_rows", 4)
-                if k % PACK == 0:
-                    z_rows[k // PACK] = ring.tile([P, PACK, J], F32, name="z_rows", tag="wide", bufs=5, align_bytes=64)
-            for h in range(2):
-                if i < tiles:
-                    first_stage(a_rows[i], h, w1_q[i // PACK], i % PACK, v1)
-                if k >= 0:
-                    first_stage(d_rows[k], h, w3_q[k // PACK], k % PACK, v3, scale=neg_keel[:, k : k + 1])
-            if i < whole:
-                fits[i] = ring.tile([P, J], F32, name="fit", tag="fit", bufs=3, align_bytes=64)
-                pick_a(i, a_rows[i], fits[i][:], every)
-            if 0 <= k < whole:
-                pick_d(k, d_rows[k], fits[k][:], every)
-            if i < whole:
-                smaller(i, fits[i][:], every)
-            if i == 2:
+        for i in range(TILES + 1):
+            before = i - 1
+            if i < TILES:
+                a_rows[i] = rotate([P, S], F32, "a_rows", "a_rows", A_BUFS)
+            if before >= 0:
+                d_rows[before] = rotate([P, S], F32, "d_rows", "d_rows", D_BUFS)
+                if before % PACK == 0:
+                    z_rows[before // PACK] = rotate([P, PACK, J], F32, "z_rows", "wide", WIDE_BUFS)
+            for which, bank in a_first if before == 0 else in_turn:
+                if which == "a" and i < TILES:
+                    first_stage(a_rows[i], bank, w1_q[i // PACK], i % PACK, v)
+                if which == "d" and before >= 0:
+                    scale = neg_keel[:, before : before + 1]
+                    first_stage(d_rows[before], bank, w3_q[before // PACK], before % PACK, v3, scale=scale)
+            if i < WHOLE_TILES:
+                fits[i] = rotate([P, J], F32, "fit", "fit", FIT_BUFS)
+                pick_a(i, fits[i][:], every)
+            if 0 <= before < WHOLE_TILES:
+                pick_d(before, fits[before][:], every)
+            if i < WHOLE_TILES:
+                take_min(i, fits[i][:], every)
+            if i == W3_LATE_STEP:
                 w3_q[1] = [quantise_weight(w3_raw[1], "w3_1")]
-        codes, plane = quantise_z(0, every, nc.scalar, "z0")
-        for h in range(2):
-            z_q[0, h] = (codes[:, HALF * h : HALF * (h + 1)], plane[:, HALF * h : HALF * (h + 1)])
-        for h in range(2):
-            cols = slice(HALF * h, HALF * (h + 1))
-            pair = ring.tile([P, 2, HALF], F32, name="pair", tag="pair", bufs=1, align_bytes=64)
-            for u in range(2):
-                pick_a(whole + u, a_rows[whole + u], pair[:, u, :], cols)
-            for u in range(2):
-                smaller(whole + u, pair[:, u, :], cols)
-            for u in range(2):
-                pick_d(whole + u, d_rows[whole + u], pair[:, u, :], cols)
-            codes, plane = quantise_z(1, cols, nc.scalar if h == 0 else nc.vector, "z1%d" % h)
-            z_q[1, h] = (codes[:], plane[:])
-            second_stage(h)
+
+        codes, plane = quantise_z(0, every, nc.scalar.copy, "z_0")
+        for half in range(2):
+            cols = slice(HALF * half, HALF * (half + 1))
+            z_q[0, half] = (codes[:, cols], plane[:, cols])
+
+        for half, copy in enumerate((nc.scalar.copy, nc.vector.tensor_copy)):
+            cols = slice(HALF * half, HALF * (half + 1))
+            last_fits = rotate([P, TILES - WHOLE_TILES, HALF], F32, "last_fits", "last_fits", 1)
+            for step in (pick_a, take_min, pick_d):
+                for i in range(WHOLE_TILES, TILES):
+                    step(i, last_fits[:, i - WHOLE_TILES, :], cols)
+            codes, plane = quantise_z(1, cols, copy, "z_1%d" % half)
+            z_q[1, half] = (codes[:], plane[:])
+            second_stage(half)

from contextlib import ExitStack

import concourse.mybir as mybir

K, K2, H, N, T, S, J = 1024, 512, 1024, 512, 2048, 1024, 512
FLOPS = 2 * (K * H * S + 2 * K2 * H * S + H * N * J)

F32 = mybir.dt.float32
BF16 = mybir.dt.bfloat16
I32 = mybir.dt.int32
U32 = mybir.dt.uint32
U16 = mybir.dt.uint16
U8 = mybir.dt.uint8
FP8X4 = mybir.dt.float8_e4m3fn_x4
FP4X4 = mybir.dt.float4_e2m1fn_x4
ALU = mybir.AluOpType
ACT = mybir.ActivationFunctionType

P = 128
PACK = 4
PASS = P * PACK
BANK = 512
HALF = J // 2
PER_COLUMN = 16
LINE = 4
TILES = H // P
WHOLE_TILES = TILES - 2

WIDE_BUFS = 5
GROUPED_BUFS = 3
A_BUFS, B_BUFS, D_BUFS = 3, 6, 4
PICKED_BUFS = TILES
FIT_BUFS = 3
ACC_BUFS = 4
W3_LATE_STEP = 2


def tile_list_berth_tide_features_kernel(
    tc, tab_words, tab_scales, tab2_words, tab2_scales, tab3_words, tab3_scales,
    offs, offs2, offs3, pos1, pos2, pos3, w1, w2_words, w2_scales, w3, ask, keel,
    w4_words, w4_scales, out,
):
    nc = tc.nc
    with ExitStack() as ctx:
        held = ctx.enter_context(tc.tile_pool(name="held", bufs=1))
        ring = ctx.enter_context(tc.tile_pool(name="ring", bufs=1))
        psum = ctx.enter_context(tc.psum_pool(name="psum", bufs=ACC_BUFS))

        def keep(shape, dtype, name):
            return held.tile(shape, dtype, name=name, align_bytes=64)

        def rotate(shape, dtype, name, tag, bufs):
            return ring.tile(shape, dtype, name=name, tag=tag, bufs=bufs, align_bytes=64)

        def load_list(src, name):
            tile = held.tile(list(src.shape), U16, name=name)
            nc.sync.dma_start(tile[:], src)
            return tile

        def entries(offsets, cols):
            return offsets[:, cols.start // PER_COLUMN : cols.stop // PER_COLUMN]

        def zeroed_plane(engine, width, name):
            tile = keep([P, width], U8, name)
            engine.memset(tile[:].bitcast(I32), 0)
            return tile

        def load_plane(plane, rows):
            for r in range(4):
                nc.sync.dma_start(out=plane[r:P:32].bitcast(I32), in_=rows[r:16:4].bitcast(I32))

        def load_two_planes(plane, scales):
            for q in range(4):
                nc.sync.dma_start(
                    out=plane[32 * q : 32 * q + 8, :].bitcast(I32),
                    in_=scales[:, 4 * q : 4 * q + 4, :].bitcast(I32),
                )

        def load_words(words, name):
            tile = keep([P, words.shape[1]], I32, name)
            nc.sync.dma_start(out=tile[:], in_=words.rearrange("p c i -> p (c i)").bitcast(I32))
            return tile

        def load_weight(rows, name):
            tile = rotate([P, PACK, BANK], F32, name, "wide", WIDE_BUFS)
            nc.sync.dma_start(out=tile[:], in_=rows.rearrange("(p i) c -> p i c", i=PACK))
            return tile

        def load_ask(g):
            rows = ask[PASS * g : PASS * (g + 1), :]
            nc.sync.dma_start(out=ask_sb[g][:], in_=rows.rearrange("(p t) j -> p t j", t=PACK))

        tab2_plane = zeroed_plane(nc.gpsimd, T, "tab2_plane")
        w2_plane_raw = zeroed_plane(nc.gpsimd, H, "w2_plane_raw")
        tab_plane = zeroed_plane(nc.vector, T, "tab_plane")
        tab3_plane = zeroed_plane(nc.vector, T, "tab3_plane")
        w4_plane = zeroed_plane(nc.vector, 2 * N, "w4_plane")

        idx2 = load_list(offs2, "idx2")
        idx = load_list(offs, "idx")
        load_plane(tab2_plane[:], tab2_scales[0])
        tab2_sb = load_words(tab2_words[0], "tab2_sb")
        tab_sb = [load_words(tab_words[0], "tab_sb0")]
        load_plane(w2_plane_raw[:], w2_scales[0])
        w2_raw = load_words(w2_words[0], "w2_raw")
        load_two_planes(tab_plane, tab_scales)
        tab_sb.append(load_words(tab_words[1], "tab_sb1"))
        p2 = load_list(pos2, "p2")
        w1_raw = {0: [load_weight(w1[PASS * c : PASS * (c + 1), 0:BANK], "w1_raw") for c in range(2)]}
        load_plane(tab3_plane[:], tab3_scales[0])
        idx3 = load_list(offs3, "idx3")
        w3_raw = {0: load_weight(w3[:, 0:BANK], "w3_raw")}
        w1_raw[1] = [load_weight(w1[PASS * c : PASS * (c + 1), BANK:H], "w1_raw") for c in range(2)]
        tab3_sb = load_words(tab3_words[0], "tab3_sb")
        p1 = load_list(pos1, "p1")
        keel_sb = keep([P, 2, PACK], F32, "keel_sb")
        nc.sync.dma_start(out=keel_sb[:], in_=keel.rearrange("(g p t) -> p g t", g=2, t=PACK))
        ask_sb = [keep([P, PACK, J], F32, "ask_sb%d" % g) for g in range(2)]
        load_ask(0)
        p3 = load_list(pos3, "p3")
        w3_raw[1] = load_weight(w3[:, BANK:H], "w3_raw")
        load_ask(1)
        w4_sb = keep([P, 2, 2 * N], U8, "w4_sb")
        nc.sync.dma_start(out=w4_sb[:].bitcast(I32), in_=w4_words.rearrange("g p c -> p g c").bitcast(I32))
        load_plane(w4_plane[:].rearrange("p (g c) -> p g c", g=2), w4_scales.rearrange("g q c -> q g c"))

        neg_keel = keep([P, TILES], F32, "neg_keel")
        nc.gpsimd.tensor_scalar(neg_keel[:], keel_sb[:].rearrange("p g t -> p (g t)"), -1.0, 0.0, ALU.mult, ALU.add)

        def gather_plane(plane, offsets, name):
            tile = keep([P, S], U8, name)
            nc.vector.tensor_copy(tile[:], plane[:].indirect(offsets[:]))
            return tile

        def gather_words(words, offsets, name, width):
            tile = keep([P, S], U32, name)
            for start in range(0, S, width):
                cols = slice(start, start + width)
                nc.vector.tensor_copy(tile[:, cols], words[:].bitcast(U32).indirect(entries(offsets, cols)))
            return tile

        def quantise(grouped, width, name):
            codes = keep([P, width], U32, name + "_codes")
            plane = keep([P, width], U8, name + "_plane")
            nc.vector.quantize_mx(out=codes[:].bitcast(FP8X4), scales=plane[:], in_=grouped[:])
            return codes, plane

        def quantise_weight(raw, name):
            grouped = rotate([P, PACK * BANK], BF16, "grouped", "grouped", GROUPED_BUFS)
            nc.scalar.copy(
                out=grouped[:].rearrange("p (t m i) -> p m i t", t=PACK, i=PACK),
                in_=raw[:].rearrange("p i (m t) -> p m i t", t=PACK),
            )
            return quantise(grouped, BANK, name)

        def first_stage(rows, bank, weight, t, looked_up, scale=None):
            stationary = slice(P * t, P * (t + 1))
            cols = slice(BANK * bank, BANK * (bank + 1))
            acc = psum.tile([P, BANK], F32, name="acc", tag="acc")
            for c, ((codes, plane), (words, words_plane)) in enumerate(zip(weight, looked_up)):
                nc.tensor.matmul_mx(
                    out=acc[:], lhsT=codes[:, stationary].bitcast(FP8X4), lhsT_scale=plane[:, stationary],
                    rhs=words[:, cols].bitcast(FP8X4), rhs_scale=words_plane[4 * c : P, cols],
                    start=(c == 0), stop=(c == len(weight) - 1),
                )
            if scale is None:
                nc.scalar.copy(out=rows[:, cols], in_=acc[:])
            else:
                nc.scalar.activation(out=rows[:, cols], in_=acc[:], func=ACT.Copy, scale=scale)

        w2_q = []
        for g in range(2):
            cols = slice(BANK * g, BANK * (g + 1))
            codes = keep([P, BANK], U32, "w2_codes%d" % g)
            plane = keep([P, BANK], U8, "w2_plane%d" % g)
            nc.scalar.copy(
                out=codes[:].rearrange("p (t u v) -> p u t v", t=PACK, v=LINE),
                in_=w2_raw[:, cols].bitcast(U32).rearrange("p (u v t) -> p u t v", t=PACK, v=LINE),
            )
            nc.gpsimd.tensor_copy(
                out=plane[:].rearrange("p (t m) -> p t m", t=PACK),
                in_=w2_plane_raw[:, cols].rearrange("p (m t) -> p t m", t=PACK),
            )
            w2_q.append([(codes, plane)])

        v2_plane = gather_plane(tab2_plane, idx2, "v2_plane")
        v2 = [(gather_words(tab2_sb, idx2, "v2_words", BANK), v2_plane)]

        b_picked = {}

        def make_and_pick_b(i):
            rows = rotate([P, S], F32, "b_rows", "b_rows", B_BUFS)
            for bank in range(S // BANK):
                first_stage(rows, bank, w2_q[i // PACK], i % PACK, v2)
            b_picked[i] = rotate([P, J], F32, "picked", "picked", PICKED_BUFS)
            nc.vector.tensor_copy(b_picked[i][:], rows[:].indirect(p2[:]))

        v_plane = gather_plane(tab_plane, idx, "v_plane")
        v = [(gather_words(tab_sb[c], idx, "v_words%d" % c, S), v_plane) for c in range(2)]
        w1_q = {0: [quantise_weight(w1_raw[0][c], "w1_0%d" % c) for c in range(2)]}
        for i in range(B_BUFS):
            make_and_pick_b(i)
        w3_q = {0: [quantise_weight(w3_raw[0], "w3_0")]}
        for i in range(B_BUFS, TILES):
            make_and_pick_b(i)
        w1_q[1] = [quantise_weight(w1_raw[1][c], "w1_1%d" % c) for c in range(2)]
        v3_plane = gather_plane(tab3_plane, idx3, "v3_plane")
        v3 = [(gather_words(tab3_sb, idx3, "v3_words", S), v3_plane)]

        z_rows = {}
        z_q = {}

        def quantise_z(g, cols, copy, name):
            width = cols.stop - cols.start
            grouped = rotate([P, PACK * width], BF16, "grouped", "grouped", GROUPED_BUFS)
            copy(
                out=grouped[:].rearrange("p (u v t) -> p u t v", t=PACK, v=LINE),
                in_=z_rows[g][:, :, cols].rearrange("p t (u v) -> p u t v", v=LINE),
            )
            return quantise(grouped, width, name)

        def second_stage(half):
            for pair_of_tiles in range(N // (2 * P)):
                acc = psum.tile([P, 2, HALF], F32, name="y_acc", tag="y_acc")
                for g in range(2):
                    codes, plane = z_q[g, half]
                    for u in range(2):
                        n = 2 * pair_of_tiles + u
                        nc.tensor.matmul_mx(
                            out=acc[:, u, :],
                            lhsT=w4_sb[:, g, 2 * P * n : 2 * P * (n + 1)].bitcast(FP4X4),
                            lhsT_scale=w4_plane[:, N * g + P * n : N * g + P * (n + 1)],
                            rhs=codes.bitcast(FP8X4), rhs_scale=plane,
                            start=(g == 0 and u == 0), stop=(g == 1 and u == 1),
                        )
                tanh_y = rotate([P, 2, HALF], F32, "tanh_y", "fit", FIT_BUFS)
                nc.scalar.activation(out=tanh_y[:], in_=acc[:], func=ACT.Tanh)
                result = rotate([P, 2, HALF], F32, "result", "picked", PICKED_BUFS)
                nc.vector.tensor_tensor(result[:], acc[:], tanh_y[:], ALU.add)
                rows = out[2 * P * pair_of_tiles : 2 * P * (pair_of_tiles + 1), HALF * half : HALF * (half + 1)]
                nc.sync.dma_start(out=rows.rearrange("(u p) j -> p u j", u=2), in_=result[:])

        a_rows = {}
        d_rows = {}

        def pick_a(i, fit, cols):
            window = a_rows[i][:].indirect(entries(p1, cols))
            nc.vector.tensor_tensor(fit, window, ask_sb[i // PACK][:, i % PACK, cols], ALU.add)

        def take_min(i, fit, cols):
            nc.vector.tensor_tensor(fit, fit, b_picked[i][:, cols], ALU.min)

        def pick_d(i, fit, cols):
            window = d_rows[i][:].indirect(entries(p3, cols))
            nc.vector.tensor_tensor(z_rows[i // PACK][:, i % PACK, cols], window, fit, ALU.add)

        in_turn = [("a", 0), ("d", 0), ("a", 1), ("d", 1)]
        a_first = [("a", 0), ("a", 1), ("d", 0), ("d", 1)]
        fits = {}
        every = slice(0, J)
        for i in range(TILES + 1):
            before = i - 1
            if i < TILES:
                a_rows[i] = rotate([P, S], F32, "a_rows", "a_rows", A_BUFS)
            if before >= 0:
                d_rows[before] = rotate([P, S], F32, "d_rows", "d_rows", D_BUFS)
                if before % PACK == 0:
                    z_rows[before // PACK] = rotate([P, PACK, J], F32, "z_rows", "wide", WIDE_BUFS)
            for which, bank in a_first if before == 0 else in_turn:
                if which == "a" and i < TILES:
                    first_stage(a_rows[i], bank, w1_q[i // PACK], i % PACK, v)
                if which == "d" and before >= 0:
                    scale = neg_keel[:, before : before + 1]
                    first_stage(d_rows[before], bank, w3_q[before // PACK], before % PACK, v3, scale=scale)
            if i < WHOLE_TILES:
                fits[i] = rotate([P, J], F32, "fit", "fit", FIT_BUFS)
                pick_a(i, fits[i][:], every)
            if 0 <= before < WHOLE_TILES:
                pick_d(before, fits[before][:], every)
            if i < WHOLE_TILES:
                take_min(i, fits[i][:], every)
            if i == W3_LATE_STEP:
                w3_q[1] = [quantise_weight(w3_raw[1], "w3_1")]

        codes, plane = quantise_z(0, every, nc.scalar.copy, "z_0")
        for half in range(2):
            cols = slice(HALF * half, HALF * (half + 1))
            z_q[0, half] = (codes[:, cols], plane[:, cols])

        for half, copy in enumerate((nc.scalar.copy, nc.vector.tensor_copy)):
            cols = slice(HALF * half, HALF * (half + 1))
            last_fits = rotate([P, TILES - WHOLE_TILES, HALF], F32, "last_fits", "last_fits", 1)
            for step in (pick_a, take_min, pick_d):
                for i in range(WHOLE_TILES, TILES):
                    step(i, last_fits[:, i - WHOLE_TILES, :], cols)
            codes, plane = quantise_z(1, cols, copy, "z_1%d" % half)
            z_q[1, half] = (codes[:], plane[:])
            second_stage(half)
